import numpy as np
import ml_dtypes


def mxq(x, axis, fmt="e4m3"):
    dtype, down = {"e4m3": (ml_dtypes.float8_e4m3fn, 7), "e5m2": (ml_dtypes.float8_e5m2, 14)}[fmt]
    v = np.moveaxis(np.asarray(x, np.float32).astype(ml_dtypes.bfloat16).astype(np.float64), axis, -1)
    blocks = v.reshape(v.shape[:-1] + (-1, 32))
    amax = np.abs(blocks).max(-1, keepdims=True)
    byte = np.maximum(np.where(amax > 0, np.frexp(amax)[1] - 1 + 127, 0) - down, 1)
    scale = np.exp2(byte - 127.0)
    codes = (blocks / scale).astype(np.float32).astype(dtype).astype(np.float64)
    return np.moveaxis((codes * scale).reshape(v.shape), -1, axis)


WIDE = False


def mx_kscale(k):
    if not WIDE:
        return np.ones(k)
    levels = np.array([10, -10, 5, -5, 0])
    if k % 512:
        return np.exp2(np.random.permutation(np.resize(levels, k // 32))).repeat(32)
    a = np.empty((k // 512, 16))
    for p in range(k // 512):
        a[p, :8] = np.random.permutation(np.resize(levels, 8))
        for g in range(8):
            far = levels[np.abs(levels - a[p, g]) >= 10]
            a[p, g + 8] = far[np.random.randint(len(far))]
    return np.exp2(a.ravel()).repeat(32)


def f64(x):
    return np.asarray(x).astype(np.float64)


def striped(idx):
    return np.tile(idx.reshape(-1, 16).T, (8, 1)).astype(np.uint16)


def unstriped(offs):
    return offs[:16].T.reshape(-1).astype(np.int64)


def pack_weight(w):
    k, n = w.shape
    w = f64(np.asarray(w, np.float32).astype(ml_dtypes.bfloat16)).reshape(k // 32, 32, n)
    amax = np.abs(w).max(1)
    byte = np.clip(np.where(amax > 0, np.frexp(amax)[1] - 1 + 127 - 7, 1), 1, 254)
    scaled = (w * np.exp2(127.0 - byte)[:, None, :]).reshape(k, n).astype(np.float32)
    words = np.ascontiguousarray(scaled.reshape(k // 512, 128, 4, n).transpose(0, 1, 3, 2)).astype(ml_dtypes.float8_e4m3fn).view(np.uint8)
    return words, np.ascontiguousarray(byte.astype(np.uint8).reshape(k // 512, 16, n))


def unpack_weight(words, scales):
    g, p, n, _ = words.shape
    vals = np.ascontiguousarray(words).view(ml_dtypes.float8_e4m3fn).astype(np.float64) * np.repeat(np.exp2(scales.astype(np.float64) - 127.0), 8, axis=1)[..., None]
    return vals.transpose(0, 1, 3, 2).reshape(g * 512, n)


E2M1 = np.array([0.0, 0.5, 1.0, 1.5, 2.0, 3.0, 4.0, 6.0, -0.0, -0.5, -1.0, -1.5, -2.0, -3.0, -4.0, -6.0])


def pack_fp4(w):
    k, n = w.shape
    w = f64(np.asarray(w, np.float32).astype(ml_dtypes.bfloat16)).reshape(k // 32, 32, n)
    amax = np.abs(w).max(1)
    mant, ex = np.frexp(amax / 6.0)
    byte = np.clip(np.where(amax > 0, np.where(mant > 0.5, ex, ex - 1) + 127, 1), 1, 254)
    scaled = (w * np.exp2(127.0 - byte)[:, None, :]).reshape(k, n).astype(np.float32)
    c = np.ascontiguousarray(scaled.reshape(k // 512, 128, 4, n).transpose(0, 1, 3, 2)).astype(ml_dtypes.float4_e2m1fn).view(np.uint8) & 0xF
    words = (c[..., 0::2] | (c[..., 1::2] << 4)).reshape(k // 512, 128, 2 * n)
    return np.ascontiguousarray(words), np.ascontiguousarray(byte.astype(np.uint8).reshape(k // 512, 16, n))


def unpack_fp4(words, scales):
    g, _, n = scales.shape
    words = np.ascontiguousarray(words).reshape(g, 128, n, 2)
    nib = np.empty((g, 128, n, 4), np.uint8)
    nib[..., 0::2] = words & 0xF
    nib[..., 1::2] = words >> 4
    vals = E2M1[nib] * np.repeat(np.exp2(scales.astype(np.float64) - 127.0), 8, axis=1)[..., None]
    return vals.transpose(0, 1, 3, 2).reshape(g * 512, n)


def planes(y):
    n, m = y.shape
    v = y.astype(np.float32).astype(ml_dtypes.bfloat16).astype(np.float64).reshape(n // 32, 32, m)
    top = np.abs(v).max(1)
    byte = np.clip(np.where(top > 0, np.frexp(top)[1] - 1 + 127 - 7, 1), 1, 254)
    codes = (v * np.exp2(127.0 - byte)[:, None, :]).reshape(n, m).astype(np.float32).astype(ml_dtypes.float8_e4m3fn).view(np.uint8)
    words = codes.reshape(n // 512, 128, 4, m).transpose(0, 1, 3, 2)
    return np.ascontiguousarray(words), np.ascontiguousarray(byte.astype(np.uint8).reshape(n // 512, 16, m))


K, T, S, N, H, U = 1024, 2048, 512, 512, 512, 1024


def setup_inputs():
    n = np.random.standard_normal
    s = mx_kscale(K)[:, None]
    u = mx_kscale(H)
    packed_xT = pack_weight(n((K, T)) * s)
    packed_w1 = pack_fp4(n((K, N)) / np.sqrt(K) / s)
    packed_w2 = pack_fp4(n((K, N)) / np.sqrt(K) / s)
    packed_w3 = pack_fp4(n((H, N)) / np.sqrt(H) / u[:, None])
    return {
        "x_words": packed_xT[0],
        "x_scales": packed_xT[1],
        "w1_words": packed_w1[0],
        "w1_scales": packed_w1[1],
        "w2_words": packed_w2[0],
        "w2_scales": packed_w2[1],
        "unit": (np.random.uniform(0.6, 1.4, (H, 1)) * u[:, None]).astype(np.float32),
        "w3_words": packed_w3[0],
        "w3_scales": packed_w3[1],
        "offs": striped(np.random.permutation(T)[:S]),
        "el1": striped(np.random.permutation(np.concatenate([np.arange(S), np.random.randint(0, S, U - S)]))),
        "el2": striped(np.random.permutation(np.concatenate([np.arange(S), np.random.randint(0, S, U - S)]))),
    }


def reference(x_words, x_scales, w1_words, w1_scales, w2_words, w2_scales, unit, w3_words, w3_scales, offs, el1, el2):
    xq = unpack_weight(x_words, x_scales)[:, unstriped(offs)]
    y = unpack_fp4(w1_words, w1_scales).T @ xq
    y_2 = y[:, unstriped(el2)]
    z1 = unpack_fp4(w2_words, w2_scales).T @ xq
    z_1 = z1[:, unstriped(el1)]
    rule = y_2 * z_1
    z_2 = z1[:, unstriped(el2)]
    y_1 = y[:, unstriped(el1)]
    hid = f64(unit) * (np.maximum(rule, z_2) - y_1)
    out_0 = unpack_fp4(w3_words, w3_scales).T @ mxq(hid, 0, "e4m3")
    return (out_0,) + planes(out_0)

@@ -1,0 +1,273 @@
+from contextlib import ExitStack
+
+import concourse.mybir as mybir
+
+K, T, S, N, H, U = 1024, 2048, 512, 512, 512, 1024
+FLOPS = 2 * (2 * K * N * S + H * N * U)
+
+F32 = mybir.dt.float32
+BF16 = mybir.dt.bfloat16
+I32 = mybir.dt.int32
+U32 = mybir.dt.uint32
+U16 = mybir.dt.uint16
+U8 = mybir.dt.uint8
+FP8X4 = mybir.dt.float8_e4m3fn_x4
+FP4X4 = mybir.dt.float4_e2m1fn_x4
+ALU = mybir.AluOpType
+COPY = mybir.ActivationFunctionType.Copy
+
+P = 128
+PACK = 4
+PASSES = K // (P * PACK)
+QUADS = 4
+UNIT = 128
+RUN = 4
+CHUNKS = (384, 384, 128, 128)
+DEAL_DT = U16
+
+
+def tile_picked_yalloyp_max_po_kernel(
+    tc, x_words, x_scales, w1_words, w1_scales, w2_words, w2_scales, unit, w3_words, w3_scales,
+    offs, el1, el2, out_0, out_1, out_2,
+):
+    nc = tc.nc
+    with ExitStack() as ctx:
+        lists = ctx.enter_context(tc.tile_pool(name="lists", bufs=1))
+        keep = ctx.enter_context(tc.tile_pool(name="keep", bufs=1))
+        psum = ctx.enter_context(tc.psum_pool(name="psum", bufs=8))
+
+        def sb(name, shape, dtype):
+            return keep.tile(shape, dtype, name=name, align_bytes=64)
+
+        def load_scale_rows(queue, plane, scales):
+            passes = scales.shape[0]
+            for q in range(QUADS):
+                queue.dma_start(
+                    out=plane[32 * q : 32 * q + 4, : passes * scales.shape[2]].bitcast(I32).rearrange("r (o c) -> r o c", o=passes),
+                    in_=scales[:, 4 * q : 4 * q + 4, :].bitcast(I32).rearrange("o r c -> r o c"),
+                )
+
+        def load_fp4_words(queue, raw, words):
+            queue.dma_start(
+                out=raw[:, : words.shape[0] * words.shape[2]].bitcast(I32).rearrange("p (o c) -> p o c", o=words.shape[0]),
+                in_=words.bitcast(I32).rearrange("o p c -> p o c"),
+            )
+
+        offs_sb = lists.tile([P, S // 16], U16, name="offs_sb")
+        el1_sb = lists.tile([P, U // 16], U16, name="el1_sb")
+        el2_sb = lists.tile([P, U // 16], U16, name="el2_sb")
+
+        xs_table = sb("xs_table", [P, PASSES * T], U8)
+        ws_raw = [sb("w1s_raw", [P, PASSES * N], U8), sb("w2s_raw", [P, PASSES * N], U8)]
+        nc.vector.memset(xs_table[:].bitcast(I32), 0)
+        nc.gpsimd.memset(ws_raw[0][:].bitcast(I32), 0)
+        nc.vector.memset(ws_raw[1][:].bitcast(I32), 0)
+
+        xw_table = [sb("xw_table%d" % o, [P, T], U32) for o in range(PASSES)]
+        ww_raw = [sb("w1w_raw", [P, PASSES * 2 * N], U8), sb("w2w_raw", [P, PASSES * 2 * N], U8)]
+        unit_sb = sb("unit_sb", [P, PACK], F32)
+
+        def load_x_words(o):
+            nc.sync.dma_start(out=xw_table[o][:].bitcast(I32), in_=x_words[o].rearrange("p c r -> p (c r)").bitcast(I32))
+
+        nc.sync.dma_start(offs_sb[:], offs)
+        load_fp4_words(nc.sync, ww_raw[1], w2_words)
+        load_scale_rows(nc.sync, xs_table, x_scales)
+        load_x_words(0)
+        load_fp4_words(nc.sync, ww_raw[0], w1_words)
+        load_x_words(1)
+        load_scale_rows(nc.sync, ws_raw[1], w2_scales)
+        load_scale_rows(nc.gpsimd, ws_raw[0], w1_scales)
+        nc.sync.dma_start(el1_sb[:], el1)
+        nc.sync.dma_start(el2_sb[:], el2)
+        nc.sync.dma_start(out=unit_sb[:], in_=unit.rearrange("(p t) o -> p (t o)", t=PACK))
+
+        xq_scales = [sb("xq_scales%d" % o, [P, S], U8) for o in range(PASSES)]
+        xq_words = [sb("xq_words%d" % o, [P, S], U32) for o in range(PASSES)]
+
+        def gather_x_scales(o):
+            nc.vector.tensor_copy(xq_scales[o][:], xs_table[:, o * T : (o + 1) * T].indirect(offs_sb[:]))
+
+        def gather_x_words(o):
+            nc.vector.tensor_copy(xq_words[o][:], xw_table[o][:].indirect(offs_sb[:]))
+
+        dealt = {}
+
+        def deal(w, half):
+            passes = PASSES if w < 2 else 1
+            words = sb("words%d_%d" % (w, half), [P, 2 * passes * P * 2], U8)
+            scales = sb("scales%d_%d" % (w, half), [P, 2 * passes * P], U8)
+            ts = slice(2 * half, 2 * half + 2)
+            nc.vector.tensor_copy(
+                out=words[:].bitcast(DEAL_DT).rearrange("p (t o m) -> p t o m", t=2, o=passes),
+                in_=ww_raw[min(w, 1)][:, : passes * 2 * N].bitcast(DEAL_DT).rearrange("p (o m t) -> p t o m", o=passes, t=PACK)[:, ts],
+            )
+            nc.vector.tensor_copy(
+                out=scales[:].rearrange("p (t o m) -> p t o m", t=2, o=passes),
+                in_=ws_raw[min(w, 1)][:, : passes * N].rearrange("p (o m t) -> p t o m", o=passes, t=PACK)[:, ts],
+            )
+            for t in range(2):
+                for o in range(passes):
+                    j = t * passes + o
+                    dealt[w, 2 * half + t, o] = (words[:, 2 * P * j : 2 * P * (j + 1)], scales[:, P * j : P * (j + 1)])
+
+        banks = {}
+
+        def project(w, t, o):
+            if o == 0:
+                banks[w, t] = psum.tile([P, S], F32, name="bank", tag="bank")
+            words, scales = dealt[w, t, o]
+            nc.tensor.matmul_mx(
+                out=banks[w, t][:], lhsT=words.bitcast(FP4X4), lhsT_scale=scales,
+                rhs=xq_words[o][:].bitcast(FP8X4), rhs_scale=xq_scales[o][:],
+                start=(o == 0), stop=(o == PASSES - 1),
+            )
+
+        neg_y = [sb("neg_y%d" % t, [P, S], F32) for t in range(PACK)]
+        z = [sb("z%d" % t, [P, S], F32) for t in range(PACK)]
+
+        def evac_y(t):
+            nc.vector.tensor_scalar(neg_y[t][:], banks[0, t][:], -1.0, None, ALU.mult)
+
+        def evac_z(t, on_vector):
+            if on_vector:
+                nc.vector.tensor_copy(z[t][:], banks[1, t][:])
+            else:
+                nc.scalar.copy(z[t][:], banks[1, t][:])
+
+        gather_x_scales(0)
+        gather_x_scales(1)
+        gather_x_words(0)
+        deal(1, 0)
+        deal(0, 0)
+        for w in (1, 0):
+            for t in range(2):
+                project(w, t, 0)
+        gather_x_words(1)
+        for t in range(2):
+            project(1, t, 1)
+            project(0, t, 1)
+        deal(1, 1)
+        deal(0, 1)
+        load_fp4_words(nc.sync, ww_raw[1], w3_words)
+        load_scale_rows(nc.sync, ws_raw[1], w3_scales)
+        for t in range(2, PACK):
+            for w in (1, 0):
+                project(w, t, 0)
+                project(w, t, 1)
+
+        starts = [sum(CHUNKS[:c]) for c in range(len(CHUNKS))]
+        z_1 = [sb("z_1_%d" % c, [P, PACK, n], F32) for c, n in enumerate(CHUNKS)]
+        z_2 = [sb("z_2_%d" % c, [P, PACK, n], F32) for c, n in enumerate(CHUNKS)]
+        neg_rule = [sb("neg_rule%d" % c, [P, PACK, n], F32) for c, n in enumerate(CHUNKS)]
+        larger = [sb("larger%d" % c, [P, PACK, n], F32) for c, n in enumerate(CHUNKS)]
+        diff = [sb("diff%d" % c, [P, PACK, n], F32) for c, n in enumerate(CHUNKS)]
+        hid = [sb("hid%d" % c, [P, PACK * n], BF16) for c, n in enumerate(CHUNKS)]
+        hid_words = [sb("hid_words%d" % c, [P, n], U32) for c, n in enumerate(CHUNKS)]
+        hid_scales = [sb("hid_scales%d" % c, [P, n], U8) for c, n in enumerate(CHUNKS)]
+        res = [sb("res%d" % c, [P, PACK, n], F32) for c, n in enumerate(CHUNKS)]
+        res_bf = [sb("res_bf%d" % c, [P, PACK * n], BF16) for c, n in enumerate(CHUNKS)]
+        res_words = [sb("res_words%d" % c, [P, n], U32) for c, n in enumerate(CHUNKS)]
+        res_scales = sb("res_scales", [P, U], U8)
+
+        def entries(lst, c):
+            return lst[:, starts[c] // 16 : (starts[c] + CHUNKS[c]) // 16]
+
+        def fetch_z1(c, t):
+            nc.scalar.activation(z_1[c][:, t, :], z[t][:].indirect(entries(el1_sb, c)), COPY)
+
+        def fetch_z2(c, t):
+            nc.scalar.activation(z_2[c][:, t, :], z[t][:].indirect(entries(el2_sb, c)), COPY)
+
+        def make_rule(c, t):
+            nc.vector.tensor_tensor(neg_rule[c][:, t, :], neg_y[t][:].indirect(entries(el2_sb, c)), z_1[c][:, t, :], ALU.mult)
+
+        def take_larger(c, t):
+            nc.vector.scalar_tensor_tensor(larger[c][:, t, :], neg_rule[c][:, t, :], -1.0, z_2[c][:, t, :], ALU.mult, ALU.max)
+
+        def make_diff(c, t):
+            nc.vector.tensor_tensor(diff[c][:, t, :], neg_y[t][:].indirect(entries(el1_sb, c)), larger[c][:, t, :], ALU.add)
+
+        def scale_round(c):
+            groups = CHUNKS[c] // RUN
+            nc.vector.tensor_tensor(
+                hid[c][:].rearrange("p (g i t) -> p g t i", i=RUN, t=PACK),
+                diff[c][:].rearrange("p t (g i) -> p g t i", i=RUN),
+                unit_sb[:].unsqueeze(1).unsqueeze(3).broadcast_to([P, groups, PACK, RUN]),
+                ALU.mult,
+            )
+
+        def quantize_hid(c):
+            nc.vector.quantize_mx(out=hid_words[c][:].bitcast(FP8X4), scales=hid_scales[c][:], in_=hid[c][:])
+
+        out_rows = out_0.rearrange("(p t) r -> p t r", t=PACK)
+        out_words = out_1[0].rearrange("p c r -> p (c r)").bitcast(I32)
+
+        def properties(c):
+            for a in range(0, CHUNKS[c], UNIT):
+                cols = slice(a, a + UNIT)
+                bank = psum.tile([P, PACK, UNIT], F32, name="bank", tag="bank")
+                for t in range(PACK):
+                    words, scales = dealt[2, t, 0]
+                    nc.tensor.matmul_mx(
+                        out=bank[:, t, :], lhsT=words.bitcast(FP4X4), lhsT_scale=scales,
+                        rhs=hid_words[c][:, cols].bitcast(FP8X4), rhs_scale=hid_scales[c][:, cols],
+                        start=True, stop=True,
+                    )
+                nc.scalar.copy(
+                    res_bf[c][:, PACK * a : PACK * (a + UNIT)].rearrange("p (g i t) -> p g t i", i=RUN, t=PACK),
+                    bank[:].rearrange("p t (g i) -> p g t i", i=RUN),
+                )
+                nc.scalar.copy(res[c][:, :, cols], bank[:])
+            nc.sync.dma_start(out=out_rows[:, :, starts[c] : starts[c] + CHUNKS[c]], in_=res[c][:])
+
+        def quantize_res(c):
+            cols = slice(starts[c], starts[c] + CHUNKS[c])
+            nc.vector.quantize_mx(out=res_words[c][:].bitcast(FP8X4), scales=res_scales[:, cols], in_=res_bf[c][:])
+            nc.sync.dma_start(out=out_words[:, cols], in_=res_words[c][:].bitcast(I32))
+
+        evac_z(0, False)
+        evac_y(0)
+        evac_z(1, True)
+        evac_y(1)
+        last = len(CHUNKS) - 1
+        for c in range(len(CHUNKS)):
+            for pair in range(2):
+                ta, tb = 2 * pair, 2 * pair + 1
+                first_use = c == 0 and pair == 1
+                if first_use:
+                    evac_z(ta, False)
+                fetch_z1(c, ta)
+                if first_use:
+                    evac_z(tb, False)
+                fetch_z1(c, tb)
+                fetch_z2(c, ta)
+                fetch_z2(c, tb)
+                make_rule(c, ta)
+                make_rule(c, tb)
+                if c > 0 and pair == 0:
+                    quantize_hid(c - 1)
+                take_larger(c, ta)
+                if c == 0 and pair == 0:
+                    evac_y(2)
+                take_larger(c, tb)
+                make_diff(c, ta)
+                make_diff(c, tb)
+                if c == 0 and pair == 0:
+                    evac_y(3)
+                if c == 0 and pair == 1:
+                    deal(2, 0)
+                    deal(2, 1)
+            if c > 0:
+                properties(c - 1)
+            if c > 1:
+                quantize_res(c - 2)
+            scale_round(c)
+        quantize_hid(last)
+        properties(last)
+        quantize_res(last - 1)
+        quantize_res(last)
+        for q in range(QUADS):
+            nc.sync.dma_start(
+                out=out_2[0, 4 * q : 4 * q + 4, :].bitcast(I32), in_=res_scales[32 * q : 32 * q + 4, :].bitcast(I32)
+            )

@@ -39,9 +39,9 @@ def tile_picked_yalloyp_max_po_kernel(
         def sb(name, shape, dtype):
             return keep.tile(shape, dtype, name=name, align_bytes=64)
 
-        def load_scale_rows(queue, plane, scales):
+        def load_scale_rows(queue, plane, scales, quads=range(QUADS)):
             passes = scales.shape[0]
-            for q in range(QUADS):
+            for q in quads:
                 queue.dma_start(
                     out=plane[32 * q : 32 * q + 4, : passes * scales.shape[2]].bitcast(I32).rearrange("r (o c) -> r o c", o=passes),
                     in_=scales[:, 4 * q : 4 * q + 4, :].bitcast(I32).rearrange("o r c -> r o c"),
@@ -60,8 +60,8 @@ def tile_picked_yalloyp_max_po_kernel(
         xs_table = sb("xs_table", [P, PASSES * T], U8)
         ws_raw = [sb("w1s_raw", [P, PASSES * N], U8), sb("w2s_raw", [P, PASSES * N], U8)]
         nc.vector.memset(xs_table[:].bitcast(I32), 0)
-        nc.gpsimd.memset(ws_raw[0][:].bitcast(I32), 0)
-        nc.vector.memset(ws_raw[1][:].bitcast(I32), 0)
+        nc.gpsimd.memset(ws_raw[1][:].bitcast(I32), 0)
+        nc.vector.memset(ws_raw[0][:].bitcast(I32), 0)
 
         xw_table = [sb("xw_table%d" % o, [P, T], U32) for o in range(PASSES)]
         ww_raw = [sb("w1w_raw", [P, PASSES * 2 * N], U8), sb("w2w_raw", [P, PASSES * 2 * N], U8)]
@@ -72,11 +72,12 @@ def tile_picked_yalloyp_max_po_kernel(
 
         nc.sync.dma_start(offs_sb[:], offs)
         load_fp4_words(nc.sync, ww_raw[1], w2_words)
-        load_scale_rows(nc.sync, xs_table, x_scales)
-        load_x_words(0)
         load_fp4_words(nc.sync, ww_raw[0], w1_words)
+        load_x_words(0)
+        load_scale_rows(nc.scalar, xs_table, x_scales)
+        load_scale_rows(nc.scalar, ws_raw[1], w2_scales, (0, 1))
         load_x_words(1)
-        load_scale_rows(nc.sync, ws_raw[1], w2_scales)
+        load_scale_rows(nc.gpsimd, ws_raw[1], w2_scales, (2, 3))
         load_scale_rows(nc.gpsimd, ws_raw[0], w1_scales)
         nc.sync.dma_start(el1_sb[:], el1)
         nc.sync.dma_start(el2_sb[:], el2)
@@ -139,13 +140,13 @@ def tile_picked_yalloyp_max_po_kernel(
         gather_x_scales(1)
         gather_x_words(0)
         deal(1, 0)
-        deal(0, 0)
-        for w in (1, 0):
-            for t in range(2):
-                project(w, t, 0)
+        for t in range(2):
+            project(1, t, 0)
         gather_x_words(1)
+        deal(0, 0)
         for t in range(2):
             project(1, t, 1)
+            project(0, t, 0)
             project(0, t, 1)
         deal(1, 1)
         deal(0, 1)
@@ -182,8 +183,9 @@ def tile_picked_yalloyp_max_po_kernel(
         def make_rule(c, t):
             nc.vector.tensor_tensor(neg_rule[c][:, t, :], neg_y[t][:].indirect(entries(el2_sb, c)), z_1[c][:, t, :], ALU.mult)
 
-        def take_larger(c, t):
-            nc.vector.scalar_tensor_tensor(larger[c][:, t, :], neg_rule[c][:, t, :], -1.0, z_2[c][:, t, :], ALU.mult, ALU.max)
+        def take_larger(c, pair):
+            ts = slice(2 * pair, 2 * pair + 2)
+            nc.vector.scalar_tensor_tensor(larger[c][:, ts, :], neg_rule[c][:, ts, :], -1.0, z_2[c][:, ts, :], ALU.mult, ALU.max)
 
         def make_diff(c, t):
             nc.vector.tensor_tensor(diff[c][:, t, :], neg_y[t][:].indirect(entries(el1_sb, c)), larger[c][:, t, :], ALU.add)
@@ -230,44 +232,45 @@ def tile_picked_yalloyp_max_po_kernel(
         evac_y(0)
         evac_z(1, True)
         evac_y(1)
+        steps = [(c, pair) for c in range(len(CHUNKS)) for pair in range(2)]
         last = len(CHUNKS) - 1
-        for c in range(len(CHUNKS)):
-            for pair in range(2):
-                ta, tb = 2 * pair, 2 * pair + 1
-                first_use = c == 0 and pair == 1
-                if first_use:
-                    evac_z(ta, False)
-                fetch_z1(c, ta)
-                if first_use:
-                    evac_z(tb, False)
-                fetch_z1(c, tb)
-                fetch_z2(c, ta)
-                fetch_z2(c, tb)
-                make_rule(c, ta)
-                make_rule(c, tb)
-                if c > 0 and pair == 0:
-                    quantize_hid(c - 1)
-                take_larger(c, ta)
-                if c == 0 and pair == 0:
-                    evac_y(2)
-                take_larger(c, tb)
-                make_diff(c, ta)
-                make_diff(c, tb)
-                if c == 0 and pair == 0:
-                    evac_y(3)
-                if c == 0 and pair == 1:
-                    deal(2, 0)
-                    deal(2, 1)
-            if c > 0:
+        for j, (c, pair) in enumerate(steps):
+            rows = (2 * pair, 2 * pair + 1)
+            for t in rows:
+                if j == 1:
+                    evac_z(t, False)
+                fetch_z1(c, t)
+            for t in rows:
+                fetch_z2(c, t)
+            for t in rows:
+                make_rule(c, t)
+            if j == 0:
+                evac_y(2)
+                evac_y(3)
+            if pair == 1 and c > 0:
+                quantize_hid(c - 1)
                 properties(c - 1)
-            if c > 1:
-                quantize_res(c - 2)
-            scale_round(c)
+            if j > 0:
+                before, before_pair = steps[j - 1]
+                for t in (2 * before_pair, 2 * before_pair + 1):
+                    make_diff(before, t)
+            take_larger(c, pair)
+            if pair == 0 and c > 0:
+                scale_round(c - 1)
+            if j == 1:
+                deal(2, 0)
+                deal(2, 1)
+        quantize_res(0)
+        for t in (2, 3):
+            make_diff(last, t)
+        quantize_res(1)
+        scale_round(last)
+        quantize_res(last - 1)
         quantize_hid(last)
         properties(last)
-        quantize_res(last - 1)
         quantize_res(last)
         for q in range(QUADS):
-            nc.sync.dma_start(
+            queue = nc.scalar if q % 2 else nc.sync
+            queue.dma_start(
                 out=out_2[0, 4 * q : 4 * q + 4, :].bitcast(I32), in_=res_scales[32 * q : 32 * q + 4, :].bitcast(I32)
             )

@@ -21,9 +21,9 @@ PACK = 4
 PASSES = K // (P * PACK)
 QUADS = 4
 UNIT = 128
-RUN = 4
+RUN = 2
 CHUNKS = (384, 384, 128, 128)
-DEAL_DT = U16
+FUSED_CHUNKS = 2
 
 
 def tile_picked_yalloyp_max_po_kernel(
@@ -36,8 +36,8 @@ def tile_picked_yalloyp_max_po_kernel(
         keep = ctx.enter_context(tc.tile_pool(name="keep", bufs=1))
         psum = ctx.enter_context(tc.psum_pool(name="psum", bufs=8))
 
-        def sb(name, shape, dtype):
-            return keep.tile(shape, dtype, name=name, align_bytes=64)
+        def sb(name, shape, dtype, tag=None):
+            return keep.tile(shape, dtype, name=name, tag=tag or name, align_bytes=64)
 
         def load_scale_rows(queue, plane, scales, quads=range(QUADS)):
             passes = scales.shape[0]
@@ -57,11 +57,12 @@ def tile_picked_yalloyp_max_po_kernel(
         el1_sb = lists.tile([P, U // 16], U16, name="el1_sb")
         el2_sb = lists.tile([P, U // 16], U16, name="el2_sb")
 
-        xs_table = sb("xs_table", [P, PASSES * T], U8)
+        xs_table = sb("xs_table", [P, T], U8)
+        xq_scales_moved = sb("xq_scales_moved", [P, S], U8)
         ws_raw = [sb("w1s_raw", [P, PASSES * N], U8), sb("w2s_raw", [P, PASSES * N], U8)]
-        nc.vector.memset(xs_table[:].bitcast(I32), 0)
         nc.gpsimd.memset(ws_raw[1][:].bitcast(I32), 0)
         nc.vector.memset(ws_raw[0][:].bitcast(I32), 0)
+        nc.vector.memset(xq_scales_moved[:].bitcast(I32), 0)
 
         xw_table = [sb("xw_table%d" % o, [P, T], U32) for o in range(PASSES)]
         ww_raw = [sb("w1w_raw", [P, PASSES * 2 * N], U8), sb("w2w_raw", [P, PASSES * 2 * N], U8)]
@@ -71,55 +72,67 @@ def tile_picked_yalloyp_max_po_kernel(
             nc.sync.dma_start(out=xw_table[o][:].bitcast(I32), in_=x_words[o].rearrange("p c r -> p (c r)").bitcast(I32))
 
         nc.sync.dma_start(offs_sb[:], offs)
+        nc.sync.dma_start(out=xs_table[0:32, :].bitcast(I32), in_=x_scales.bitcast(I32).rearrange("o q c -> (o q) c"))
+        for q in range(1, QUADS):
+            nc.sync.dma_start(
+                out=xs_table[32 * q : 32 * (q + 1), :].bitcast(I32),
+                in_=x_scales[0, 4 * q : 4 * q + 4, :].bitcast(I32).unsqueeze(0).broadcast_to([8, 4, T // 4]),
+            )
+        load_x_words(0)
+        load_scale_rows(nc.scalar, ws_raw[1], w2_scales, (0, 1, 2))
         load_fp4_words(nc.sync, ww_raw[1], w2_words)
         load_fp4_words(nc.sync, ww_raw[0], w1_words)
-        load_x_words(0)
-        load_scale_rows(nc.scalar, xs_table, x_scales)
-        load_scale_rows(nc.scalar, ws_raw[1], w2_scales, (0, 1))
         load_x_words(1)
-        load_scale_rows(nc.gpsimd, ws_raw[1], w2_scales, (2, 3))
+        load_scale_rows(nc.gpsimd, ws_raw[1], w2_scales, (3,))
         load_scale_rows(nc.gpsimd, ws_raw[0], w1_scales)
         nc.sync.dma_start(el1_sb[:], el1)
         nc.sync.dma_start(el2_sb[:], el2)
         nc.sync.dma_start(out=unit_sb[:], in_=unit.rearrange("(p t) o -> p (t o)", t=PACK))
 
-        xq_scales = [sb("xq_scales%d" % o, [P, S], U8) for o in range(PASSES)]
+        xq_scales_both = sb("xq_scales_both", [P, S], U8)
+        xq_scales = [xq_scales_both, xq_scales_moved]
         xq_words = [sb("xq_words%d" % o, [P, S], U32) for o in range(PASSES)]
 
-        def gather_x_scales(o):
-            nc.vector.tensor_copy(xq_scales[o][:], xs_table[:, o * T : (o + 1) * T].indirect(offs_sb[:]))
+        def gather_x_scales():
+            nc.vector.tensor_copy(xq_scales_both[:], xs_table[:].indirect(offs_sb[:]))
+            for q in range(QUADS):
+                nc.scalar.dma_start(
+                    out=xq_scales_moved[32 * q : 32 * q + 4, :].bitcast(I32),
+                    in_=xq_scales_both[16 + 4 * q : 20 + 4 * q, :].bitcast(I32),
+                )
 
         def gather_x_words(o):
             nc.vector.tensor_copy(xq_words[o][:], xw_table[o][:].indirect(offs_sb[:]))
 
-        dealt = {}
+        def deal_words(name, raw, passes):
+            words = sb(name, [P, PACK * passes * P * 2], U8)
+            nc.vector.tensor_copy(
+                out=words[:].bitcast(U16).rearrange("p (t o m) -> p t o m", t=PACK, o=passes),
+                in_=raw[:, : passes * 2 * N].bitcast(U16).rearrange("p (o m t) -> p t o m", o=passes, t=PACK),
+            )
+            return words
 
-        def deal(w, half):
-            passes = PASSES if w < 2 else 1
-            words = sb("words%d_%d" % (w, half), [P, 2 * passes * P * 2], U8)
-            scales = sb("scales%d_%d" % (w, half), [P, 2 * passes * P], U8)
-            ts = slice(2 * half, 2 * half + 2)
+        def deal_scales(scales, raw, passes, pair):
             nc.vector.tensor_copy(
-                out=words[:].bitcast(DEAL_DT).rearrange("p (t o m) -> p t o m", t=2, o=passes),
-                in_=ww_raw[min(w, 1)][:, : passes * 2 * N].bitcast(DEAL_DT).rearrange("p (o m t) -> p t o m", o=passes, t=PACK)[:, ts],
+                out=scales.rearrange("p (t o m) -> p t o m", t=2, o=passes),
+                in_=raw[:, : passes * N].rearrange("p (o m t) -> p t o m", o=passes, t=PACK)[:, 2 * pair : 2 * pair + 2],
             )
-            nc.vector.tensor_copy(
-                out=scales[:].rearrange("p (t o m) -> p t o m", t=2, o=passes),
-                in_=ws_raw[min(w, 1)][:, : passes * N].rearrange("p (o m t) -> p t o m", o=passes, t=PACK)[:, ts],
-            )
-            for t in range(2):
-                for o in range(passes):
-                    j = t * passes + o
-                    dealt[w, 2 * half + t, o] = (words[:, 2 * P * j : 2 * P * (j + 1)], scales[:, P * j : P * (j + 1)])
+            return scales
+
+        def stationary(weight, t, o, passes):
+            words, scales = weight
+            j = t * passes + o
+            j_pair = (t % 2) * passes + o
+            return words[:, 2 * P * j : 2 * P * (j + 1)].bitcast(FP4X4), scales[t // 2][:, P * j_pair : P * (j_pair + 1)]
 
         banks = {}
 
-        def project(w, t, o):
+        def project(w, weight, t, o):
             if o == 0:
                 banks[w, t] = psum.tile([P, S], F32, name="bank", tag="bank")
-            words, scales = dealt[w, t, o]
+            words, scales = stationary(weight, t, o, PASSES)
             nc.tensor.matmul_mx(
-                out=banks[w, t][:], lhsT=words.bitcast(FP4X4), lhsT_scale=scales,
+                out=banks[w, t][:], lhsT=words, lhsT_scale=scales,
                 rhs=xq_words[o][:].bitcast(FP8X4), rhs_scale=xq_scales[o][:],
                 start=(o == 0), stop=(o == PASSES - 1),
             )
@@ -136,30 +149,34 @@ def tile_picked_yalloyp_max_po_kernel(
             else:
                 nc.scalar.copy(z[t][:], banks[1, t][:])
 
-        gather_x_scales(0)
-        gather_x_scales(1)
+        gather_x_scales()
         gather_x_words(0)
-        deal(1, 0)
+        w2_words_dealt = deal_words("w2_words_dealt", ww_raw[1], PASSES)
+        w2 = (w2_words_dealt, [deal_scales(sb("early_scales", [P, N], U8, "xw_table0")[:], ws_raw[1], PASSES, 0)])
         for t in range(2):
-            project(1, t, 0)
+            project(1, w2, t, 0)
+        w1_words_dealt = deal_words("w1_words_dealt", ww_raw[0], PASSES)
         gather_x_words(1)
-        deal(0, 0)
         for t in range(2):
-            project(1, t, 1)
-            project(0, t, 0)
-            project(0, t, 1)
-        deal(1, 1)
-        deal(0, 1)
+            project(1, w2, t, 1)
+        late_scales = sb("late_scales", [P, 3, N], U8, "xw_table1")
+        w1 = (w1_words_dealt, [deal_scales(late_scales[:, 0, :], ws_raw[0], PASSES, 0)])
+        for t in range(2):
+            for o in range(PASSES):
+                project(0, w1, t, o)
+        w2[1].append(deal_scales(late_scales[:, 1, :], ws_raw[1], PASSES, 1))
+        w1[1].append(deal_scales(late_scales[:, 2, :], ws_raw[0], PASSES, 1))
+        for t in range(2, PACK):
+            for w, weight in ((1, w2), (0, w1)):
+                for o in range(PASSES):
+                    project(w, weight, t, o)
         load_fp4_words(nc.sync, ww_raw[1], w3_words)
         load_scale_rows(nc.sync, ws_raw[1], w3_scales)
-        for t in range(2, PACK):
-            for w in (1, 0):
-                project(w, t, 0)
-                project(w, t, 1)
 
         starts = [sum(CHUNKS[:c]) for c in range(len(CHUNKS))]
         z_1 = [sb("z_1_%d" % c, [P, PACK, n], F32) for c, n in enumerate(CHUNKS)]
         z_2 = [sb("z_2_%d" % c, [P, PACK, n], F32) for c, n in enumerate(CHUNKS)]
+        neg_y_1 = {c: sb("neg_y_1_%d" % c, [P, PACK, CHUNKS[c]], F32) for c in range(FUSED_CHUNKS, len(CHUNKS))}
         neg_rule = [sb("neg_rule%d" % c, [P, PACK, n], F32) for c, n in enumerate(CHUNKS)]
         larger = [sb("larger%d" % c, [P, PACK, n], F32) for c, n in enumerate(CHUNKS)]
         diff = [sb("diff%d" % c, [P, PACK, n], F32) for c, n in enumerate(CHUNKS)]
@@ -187,8 +204,16 @@ def tile_picked_yalloyp_max_po_kernel(
             ts = slice(2 * pair, 2 * pair + 2)
             nc.vector.scalar_tensor_tensor(larger[c][:, ts, :], neg_rule[c][:, ts, :], -1.0, z_2[c][:, ts, :], ALU.mult, ALU.max)
 
-        def make_diff(c, t):
-            nc.vector.tensor_tensor(diff[c][:, t, :], neg_y[t][:].indirect(entries(el1_sb, c)), larger[c][:, t, :], ALU.add)
+        def fetch_y1(c, t):
+            nc.scalar.activation(neg_y_1[c][:, t, :], neg_y[t][:].indirect(entries(el1_sb, c)), COPY)
+
+        def make_diff(c, pair):
+            if c < FUSED_CHUNKS:
+                for t in (2 * pair, 2 * pair + 1):
+                    nc.vector.tensor_tensor(diff[c][:, t, :], neg_y[t][:].indirect(entries(el1_sb, c)), larger[c][:, t, :], ALU.add)
+            else:
+                ts = slice(2 * pair, 2 * pair + 2)
+                nc.vector.tensor_tensor(diff[c][:, ts, :], neg_y_1[c][:, ts, :], larger[c][:, ts, :], ALU.add)
 
         def scale_round(c):
             groups = CHUNKS[c] // RUN
@@ -205,14 +230,14 @@ def tile_picked_yalloyp_max_po_kernel(
         out_rows = out_0.rearrange("(p t) r -> p t r", t=PACK)
         out_words = out_1[0].rearrange("p c r -> p (c r)").bitcast(I32)
 
-        def properties(c):
+        def properties(c, w3):
             for a in range(0, CHUNKS[c], UNIT):
                 cols = slice(a, a + UNIT)
                 bank = psum.tile([P, PACK, UNIT], F32, name="bank", tag="bank")
                 for t in range(PACK):
-                    words, scales = dealt[2, t, 0]
+                    words, scales = stationary(w3, t, 0, 1)
                     nc.tensor.matmul_mx(
-                        out=bank[:, t, :], lhsT=words.bitcast(FP4X4), lhsT_scale=scales,
+                        out=bank[:, t, :], lhsT=words, lhsT_scale=scales,
                         rhs=hid_words[c][:, cols].bitcast(FP8X4), rhs_scale=hid_scales[c][:, cols],
                         start=True, stop=True,
                     )
@@ -229,8 +254,8 @@ def tile_picked_yalloyp_max_po_kernel(
             nc.sync.dma_start(out=out_words[:, cols], in_=res_words[c][:].bitcast(I32))
 
         evac_z(0, False)
-        evac_y(0)
         evac_z(1, True)
+        evac_y(0)
         evac_y(1)
         steps = [(c, pair) for c in range(len(CHUNKS)) for pair in range(2)]
         last = len(CHUNKS) - 1
@@ -242,6 +267,9 @@ def tile_picked_yalloyp_max_po_kernel(
                 fetch_z1(c, t)
             for t in rows:
                 fetch_z2(c, t)
+            if c >= FUSED_CHUNKS:
+                for t in rows:
+                    fetch_y1(c, t)
             for t in rows:
                 make_rule(c, t)
             if j == 0:
@@ -249,25 +277,21 @@ def tile_picked_yalloyp_max_po_kernel(
                 evac_y(3)
             if pair == 1 and c > 0:
                 quantize_hid(c - 1)
-                properties(c - 1)
+                properties(c - 1, w3)
             if j > 0:
-                before, before_pair = steps[j - 1]
-                for t in (2 * before_pair, 2 * before_pair + 1):
-                    make_diff(before, t)
+                make_diff(*steps[j - 1])
             take_larger(c, pair)
             if pair == 0 and c > 0:
                 scale_round(c - 1)
             if j == 1:
-                deal(2, 0)
-                deal(2, 1)
+                w3 = (deal_words("w3_words_dealt", ww_raw[1], 1), [deal_scales(sb("w3_scales_%d" % h, [P, 2 * P], U8)[:], ws_raw[1], 1, h) for h in range(2)])
         quantize_res(0)
-        for t in (2, 3):
-            make_diff(last, t)
+        make_diff(last, 1)
         quantize_res(1)
         scale_round(last)
         quantize_res(last - 1)
         quantize_hid(last)
-        properties(last)
+        properties(last, w3)
         quantize_res(last)
         for q in range(QUADS):
             queue = nc.scalar if q % 2 else nc.sync

@@ -23,7 +23,7 @@ QUADS = 4
 UNIT = 128
 RUN = 2
 CHUNKS = (384, 384, 128, 128)
-FUSED_CHUNKS = 2
+FUSED_STEPS = 4
 
 
 def tile_picked_yalloyp_max_po_kernel(
@@ -81,8 +81,8 @@ def tile_picked_yalloyp_max_po_kernel(
         load_x_words(0)
         load_scale_rows(nc.scalar, ws_raw[1], w2_scales, (0, 1, 2))
         load_fp4_words(nc.sync, ww_raw[1], w2_words)
-        load_fp4_words(nc.sync, ww_raw[0], w1_words)
         load_x_words(1)
+        load_fp4_words(nc.sync, ww_raw[0], w1_words)
         load_scale_rows(nc.gpsimd, ws_raw[1], w2_scales, (3,))
         load_scale_rows(nc.gpsimd, ws_raw[0], w1_scales)
         nc.sync.dma_start(el1_sb[:], el1)
@@ -104,35 +104,25 @@ def tile_picked_yalloyp_max_po_kernel(
         def gather_x_words(o):
             nc.vector.tensor_copy(xq_words[o][:], xw_table[o][:].indirect(offs_sb[:]))
 
-        def deal_words(name, raw, passes):
-            words = sb(name, [P, PACK * passes * P * 2], U8)
+        def deal(dealt, raw, passes, first, count):
             nc.vector.tensor_copy(
-                out=words[:].bitcast(U16).rearrange("p (t o m) -> p t o m", t=PACK, o=passes),
-                in_=raw[:, : passes * 2 * N].bitcast(U16).rearrange("p (o m t) -> p t o m", o=passes, t=PACK),
+                out=dealt.rearrange("p (t o m) -> p t o m", t=count, o=passes),
+                in_=raw[:, : passes * N].rearrange("p (o m t) -> p t o m", o=passes, t=PACK)[:, first : first + count],
             )
-            return words
-
-        def deal_scales(scales, raw, passes, pair):
-            nc.vector.tensor_copy(
-                out=scales.rearrange("p (t o m) -> p t o m", t=2, o=passes),
-                in_=raw[:, : passes * N].rearrange("p (o m t) -> p t o m", o=passes, t=PACK)[:, 2 * pair : 2 * pair + 2],
-            )
-            return scales
-
-        def stationary(weight, t, o, passes):
-            words, scales = weight
-            j = t * passes + o
-            j_pair = (t % 2) * passes + o
-            return words[:, 2 * P * j : 2 * P * (j + 1)].bitcast(FP4X4), scales[t // 2][:, P * j_pair : P * (j_pair + 1)]
+            return {
+                (first + i, o): dealt[:, P * (i * passes + o) : P * (i * passes + o + 1)]
+                for i in range(count)
+                for o in range(passes)
+            }
 
         banks = {}
 
         def project(w, weight, t, o):
             if o == 0:
                 banks[w, t] = psum.tile([P, S], F32, name="bank", tag="bank")
-            words, scales = stationary(weight, t, o, PASSES)
+            words, scales = weight
             nc.tensor.matmul_mx(
-                out=banks[w, t][:], lhsT=words, lhsT_scale=scales,
+                out=banks[w, t][:], lhsT=words[t, o].bitcast(U8).bitcast(FP4X4), lhsT_scale=scales[t, o],
                 rhs=xq_words[o][:].bitcast(FP8X4), rhs_scale=xq_scales[o][:],
                 start=(o == 0), stop=(o == PASSES - 1),
             )
@@ -151,21 +141,27 @@ def tile_picked_yalloyp_max_po_kernel(
 
         gather_x_scales()
         gather_x_words(0)
-        w2_words_dealt = deal_words("w2_words_dealt", ww_raw[1], PASSES)
-        w2 = (w2_words_dealt, [deal_scales(sb("early_scales", [P, N], U8, "xw_table0")[:], ws_raw[1], PASSES, 0)])
+        early = sb("early", [P, 5 * N], U8, "xw_table0")
+        w2_words_dealt = deal(early[:, : 4 * N].bitcast(U16), ww_raw[1][:].bitcast(U16), PASSES, 0, PACK)
+        w2 = (w2_words_dealt, deal(early[:, 4 * N :], ws_raw[1][:], PASSES, 0, 2))
         for t in range(2):
             project(1, w2, t, 0)
-        w1_words_dealt = deal_words("w1_words_dealt", ww_raw[0], PASSES)
         gather_x_words(1)
         for t in range(2):
             project(1, w2, t, 1)
-        late_scales = sb("late_scales", [P, 3, N], U8, "xw_table1")
-        w1 = (w1_words_dealt, [deal_scales(late_scales[:, 0, :], ws_raw[0], PASSES, 0)])
+        late = sb("late", [P, 7 * N], U8, "xw_table1")
+        w1 = (
+            deal(late[:, : 2 * N].bitcast(U16), ww_raw[0][:].bitcast(U16), PASSES, 0, 2),
+            deal(late[:, 2 * N : 3 * N], ws_raw[0][:], PASSES, 0, 2),
+        )
         for t in range(2):
             for o in range(PASSES):
                 project(0, w1, t, o)
-        w2[1].append(deal_scales(late_scales[:, 1, :], ws_raw[1], PASSES, 1))
-        w1[1].append(deal_scales(late_scales[:, 2, :], ws_raw[0], PASSES, 1))
+        w2 = (w2_words_dealt, deal(late[:, 3 * N : 4 * N], ws_raw[1][:], PASSES, 2, 2))
+        w1 = (
+            deal(late[:, 4 * N : 6 * N].bitcast(U16), ww_raw[0][:].bitcast(U16), PASSES, 2, 2),
+            deal(late[:, 6 * N :], ws_raw[0][:], PASSES, 2, 2),
+        )
         for t in range(2, PACK):
             for w, weight in ((1, w2), (0, w1)):
                 for o in range(PASSES):
@@ -176,7 +172,7 @@ def tile_picked_yalloyp_max_po_kernel(
         starts = [sum(CHUNKS[:c]) for c in range(len(CHUNKS))]
         z_1 = [sb("z_1_%d" % c, [P, PACK, n], F32) for c, n in enumerate(CHUNKS)]
         z_2 = [sb("z_2_%d" % c, [P, PACK, n], F32) for c, n in enumerate(CHUNKS)]
-        neg_y_1 = {c: sb("neg_y_1_%d" % c, [P, PACK, CHUNKS[c]], F32) for c in range(FUSED_CHUNKS, len(CHUNKS))}
+        neg_y_1 = {c: sb("neg_y_1_%d" % c, [P, PACK, CHUNKS[c]], F32) for c in range(FUSED_STEPS // 2, len(CHUNKS))}
         neg_rule = [sb("neg_rule%d" % c, [P, PACK, n], F32) for c, n in enumerate(CHUNKS)]
         larger = [sb("larger%d" % c, [P, PACK, n], F32) for c, n in enumerate(CHUNKS)]
         diff = [sb("diff%d" % c, [P, PACK, n], F32) for c, n in enumerate(CHUNKS)]
@@ -208,7 +204,7 @@ def tile_picked_yalloyp_max_po_kernel(
             nc.scalar.activation(neg_y_1[c][:, t, :], neg_y[t][:].indirect(entries(el1_sb, c)), COPY)
 
         def make_diff(c, pair):
-            if c < FUSED_CHUNKS:
+            if 2 * c + pair < FUSED_STEPS:
                 for t in (2 * pair, 2 * pair + 1):
                     nc.vector.tensor_tensor(diff[c][:, t, :], neg_y[t][:].indirect(entries(el1_sb, c)), larger[c][:, t, :], ALU.add)
             else:
@@ -235,9 +231,9 @@ def tile_picked_yalloyp_max_po_kernel(
                 cols = slice(a, a + UNIT)
                 bank = psum.tile([P, PACK, UNIT], F32, name="bank", tag="bank")
                 for t in range(PACK):
-                    words, scales = stationary(w3, t, 0, 1)
+                    words, scales = w3
                     nc.tensor.matmul_mx(
-                        out=bank[:, t, :], lhsT=words, lhsT_scale=scales,
+                        out=bank[:, t, :], lhsT=words[t, 0].bitcast(U8).bitcast(FP4X4), lhsT_scale=scales[t, 0],
                         rhs=hid_words[c][:, cols].bitcast(FP8X4), rhs_scale=hid_scales[c][:, cols],
                         start=True, stop=True,
                     )
@@ -248,10 +244,14 @@ def tile_picked_yalloyp_max_po_kernel(
                 nc.scalar.copy(res[c][:, :, cols], bank[:])
             nc.sync.dma_start(out=out_rows[:, :, starts[c] : starts[c] + CHUNKS[c]], in_=res[c][:])
 
-        def quantize_res(c):
-            cols = slice(starts[c], starts[c] + CHUNKS[c])
-            nc.vector.quantize_mx(out=res_words[c][:].bitcast(FP8X4), scales=res_scales[:, cols], in_=res_bf[c][:])
-            nc.sync.dma_start(out=out_words[:, cols], in_=res_words[c][:].bitcast(I32))
+        def quantize_res(c, a):
+            nc.vector.quantize_mx(
+                out=res_words[c][:, a : a + UNIT].bitcast(FP8X4),
+                scales=res_scales[:, starts[c] + a : starts[c] + a + UNIT],
+                in_=res_bf[c][:, PACK * a : PACK * (a + UNIT)],
+            )
+            if a + UNIT == CHUNKS[c]:
+                nc.sync.dma_start(out=out_words[:, starts[c] : starts[c] + CHUNKS[c]], in_=res_words[c][:].bitcast(I32))
 
         evac_z(0, False)
         evac_z(1, True)
@@ -267,7 +267,7 @@ def tile_picked_yalloyp_max_po_kernel(
                 fetch_z1(c, t)
             for t in rows:
                 fetch_z2(c, t)
-            if c >= FUSED_CHUNKS:
+            if j >= FUSED_STEPS:
                 for t in rows:
                     fetch_y1(c, t)
             for t in rows:
@@ -284,15 +284,21 @@ def tile_picked_yalloyp_max_po_kernel(
             if pair == 0 and c > 0:
                 scale_round(c - 1)
             if j == 1:
-                w3 = (deal_words("w3_words_dealt", ww_raw[1], 1), [deal_scales(sb("w3_scales_%d" % h, [P, 2 * P], U8)[:], ws_raw[1], 1, h) for h in range(2)])
-        quantize_res(0)
+                w3_dealt = sb("w3_dealt", [P, 3 * N], U8)
+                w3 = (
+                    deal(w3_dealt[:, : 2 * N].bitcast(U16), ww_raw[1][:].bitcast(U16), 1, 0, PACK),
+                    deal(w3_dealt[:, 2 * N :], ws_raw[1][:], 1, 0, PACK),
+                )
+        quantize_res(0, 0)
         make_diff(last, 1)
-        quantize_res(1)
+        quantize_res(0, UNIT)
         scale_round(last)
-        quantize_res(last - 1)
+        quantize_res(0, 2 * UNIT)
         quantize_hid(last)
         properties(last, w3)
-        quantize_res(last)
+        for c in range(1, len(CHUNKS)):
+            for a in range(0, CHUNKS[c], UNIT):
+                quantize_res(c, a)
         for q in range(QUADS):
             queue = nc.scalar if q % 2 else nc.sync
             queue.dma_start(

from contextlib import ExitStack

import concourse.mybir as mybir

K, T, S, N, H, U = 1024, 2048, 512, 512, 512, 1024
FLOPS = 2 * (2 * K * N * S + H * N * U)

F32 = mybir.dt.float32
BF16 = mybir.dt.bfloat16
I32 = mybir.dt.int32
U32 = mybir.dt.uint32
U16 = mybir.dt.uint16
U8 = mybir.dt.uint8
FP8X4 = mybir.dt.float8_e4m3fn_x4
FP4X4 = mybir.dt.float4_e2m1fn_x4
ALU = mybir.AluOpType
COPY = mybir.ActivationFunctionType.Copy

P = 128
PACK = 4
PASSES = K // (P * PACK)
QUADS = 4
UNIT = 128
RUN = 2
CHUNKS = (384, 384, 128, 128)
FUSED_STEPS = 4


def tile_picked_yalloyp_max_po_kernel(
    tc, x_words, x_scales, w1_words, w1_scales, w2_words, w2_scales, unit, w3_words, w3_scales,
    offs, el1, el2, out_0, out_1, out_2,
):
    nc = tc.nc
    with ExitStack() as ctx:
        lists = ctx.enter_context(tc.tile_pool(name="lists", bufs=1))
        keep = ctx.enter_context(tc.tile_pool(name="keep", bufs=1))
        psum = ctx.enter_context(tc.psum_pool(name="psum", bufs=8))

        def sb(name, shape, dtype, tag=None):
            return keep.tile(shape, dtype, name=name, tag=tag or name, align_bytes=64)

        def load_scale_rows(queue, plane, scales, quads=range(QUADS)):
            passes = scales.shape[0]
            for q in quads:
                queue.dma_start(
                    out=plane[32 * q : 32 * q + 4, : passes * scales.shape[2]].bitcast(I32).rearrange("r (o c) -> r o c", o=passes),
                    in_=scales[:, 4 * q : 4 * q + 4, :].bitcast(I32).rearrange("o r c -> r o c"),
                )

        def load_fp4_words(queue, raw, words):
            queue.dma_start(
                out=raw[:, : words.shape[0] * words.shape[2]].bitcast(I32).rearrange("p (o c) -> p o c", o=words.shape[0]),
                in_=words.bitcast(I32).rearrange("o p c -> p o c"),
            )

        offs_sb = lists.tile([P, S // 16], U16, name="offs_sb")
        el1_sb = lists.tile([P, U // 16], U16, name="el1_sb")
        el2_sb = lists.tile([P, U // 16], U16, name="el2_sb")

        xs_table = sb("xs_table", [P, T], U8)
        xq_scales_moved = sb("xq_scales_moved", [P, S], U8)
        ws_raw = [sb("w1s_raw", [P, PASSES * N], U8), sb("w2s_raw", [P, PASSES * N], U8)]
        nc.gpsimd.memset(ws_raw[1][:].bitcast(I32), 0)
        nc.vector.memset(ws_raw[0][:].bitcast(I32), 0)
        nc.vector.memset(xq_scales_moved[:].bitcast(I32), 0)

        xw_table = [sb("xw_table%d" % o, [P, T], U32) for o in range(PASSES)]
        ww_raw = [sb("w1w_raw", [P, PASSES * 2 * N], U8), sb("w2w_raw", [P, PASSES * 2 * N], U8)]
        unit_sb = sb("unit_sb", [P, PACK], F32)

        def load_x_words(o):
            nc.sync.dma_start(out=xw_table[o][:].bitcast(I32), in_=x_words[o].rearrange("p c r -> p (c r)").bitcast(I32))

        nc.sync.dma_start(offs_sb[:], offs)
        nc.sync.dma_start(out=xs_table[0:32, :].bitcast(I32), in_=x_scales.bitcast(I32).rearrange("o q c -> (o q) c"))
        for q in range(1, QUADS):
            nc.sync.dma_start(
                out=xs_table[32 * q : 32 * (q + 1), :].bitcast(I32),
                in_=x_scales[0, 4 * q : 4 * q + 4, :].bitcast(I32).unsqueeze(0).broadcast_to([8, 4, T // 4]),
            )
        load_x_words(0)
        load_scale_rows(nc.scalar, ws_raw[1], w2_scales, (0, 1, 2))
        load_fp4_words(nc.sync, ww_raw[1], w2_words)
        load_x_words(1)
        load_fp4_words(nc.sync, ww_raw[0], w1_words)
        load_scale_rows(nc.gpsimd, ws_raw[1], w2_scales, (3,))
        load_scale_rows(nc.gpsimd, ws_raw[0], w1_scales)
        nc.sync.dma_start(el1_sb[:], el1)
        nc.sync.dma_start(el2_sb[:], el2)
        nc.sync.dma_start(out=unit_sb[:], in_=unit.rearrange("(p t) o -> p (t o)", t=PACK))

        xq_scales_both = sb("xq_scales_both", [P, S], U8)
        xq_scales = [xq_scales_both, xq_scales_moved]
        xq_words = [sb("xq_words%d" % o, [P, S], U32) for o in range(PASSES)]

        def gather_x_scales():
            nc.vector.tensor_copy(xq_scales_both[:], xs_table[:].indirect(offs_sb[:]))
            for q in range(QUADS):
                nc.scalar.dma_start(
                    out=xq_scales_moved[32 * q : 32 * q + 4, :].bitcast(I32),
                    in_=xq_scales_both[16 + 4 * q : 20 + 4 * q, :].bitcast(I32),
                )

        def gather_x_words(o):
            nc.vector.tensor_copy(xq_words[o][:], xw_table[o][:].indirect(offs_sb[:]))

        def deal(dealt, raw, passes, first, count):
            nc.vector.tensor_copy(
                out=dealt.rearrange("p (t o m) -> p t o m", t=count, o=passes),
                in_=raw[:, : passes * N].rearrange("p (o m t) -> p t o m", o=passes, t=PACK)[:, first : first + count],
            )
            return {
                (first + i, o): dealt[:, P * (i * passes + o) : P * (i * passes + o + 1)]
                for i in range(count)
                for o in range(passes)
            }

        banks = {}

        def project(w, weight, t, o):
            if o == 0:
                banks[w, t] = psum.tile([P, S], F32, name="bank", tag="bank")
            words, scales = weight
            nc.tensor.matmul_mx(
                out=banks[w, t][:], lhsT=words[t, o].bitcast(U8).bitcast(FP4X4), lhsT_scale=scales[t, o],
                rhs=xq_words[o][:].bitcast(FP8X4), rhs_scale=xq_scales[o][:],
                start=(o == 0), stop=(o == PASSES - 1),
            )

        neg_y = [sb("neg_y%d" % t, [P, S], F32) for t in range(PACK)]
        z = [sb("z%d" % t, [P, S], F32) for t in range(PACK)]

        def evac_y(t):
            nc.vector.tensor_scalar(neg_y[t][:], banks[0, t][:], -1.0, None, ALU.mult)

        def evac_z(t, on_vector):
            if on_vector:
                nc.vector.tensor_copy(z[t][:], banks[1, t][:])
            else:
                nc.scalar.copy(z[t][:], banks[1, t][:])

        gather_x_scales()
        gather_x_words(0)
        early = sb("early", [P, 5 * N], U8, "xw_table0")
        w2_words_dealt = deal(early[:, : 4 * N].bitcast(U16), ww_raw[1][:].bitcast(U16), PASSES, 0, PACK)
        w2 = (w2_words_dealt, deal(early[:, 4 * N :], ws_raw[1][:], PASSES, 0, 2))
        for t in range(2):
            project(1, w2, t, 0)
        gather_x_words(1)
        for t in range(2):
            project(1, w2, t, 1)
        late = sb("late", [P, 7 * N], U8, "xw_table1")
        w1 = (
            deal(late[:, : 2 * N].bitcast(U16), ww_raw[0][:].bitcast(U16), PASSES, 0, 2),
            deal(late[:, 2 * N : 3 * N], ws_raw[0][:], PASSES, 0, 2),
        )
        for t in range(2):
            for o in range(PASSES):
                project(0, w1, t, o)
        w2 = (w2_words_dealt, deal(late[:, 3 * N : 4 * N], ws_raw[1][:], PASSES, 2, 2))
        w1 = (
            deal(late[:, 4 * N : 6 * N].bitcast(U16), ww_raw[0][:].bitcast(U16), PASSES, 2, 2),
            deal(late[:, 6 * N :], ws_raw[0][:], PASSES, 2, 2),
        )
        for t in range(2, PACK):
            for w, weight in ((1, w2), (0, w1)):
                for o in range(PASSES):
                    project(w, weight, t, o)
        load_fp4_words(nc.sync, ww_raw[1], w3_words)
        load_scale_rows(nc.sync, ws_raw[1], w3_scales)

        starts = [sum(CHUNKS[:c]) for c in range(len(CHUNKS))]
        z_1 = [sb("z_1_%d" % c, [P, PACK, n], F32) for c, n in enumerate(CHUNKS)]
        z_2 = [sb("z_2_%d" % c, [P, PACK, n], F32) for c, n in enumerate(CHUNKS)]
        neg_y_1 = {c: sb("neg_y_1_%d" % c, [P, PACK, CHUNKS[c]], F32) for c in range(FUSED_STEPS // 2, len(CHUNKS))}
        neg_rule = [sb("neg_rule%d" % c, [P, PACK, n], F32) for c, n in enumerate(CHUNKS)]
        larger = [sb("larger%d" % c, [P, PACK, n], F32) for c, n in enumerate(CHUNKS)]
        diff = [sb("diff%d" % c, [P, PACK, n], F32) for c, n in enumerate(CHUNKS)]
        hid = [sb("hid%d" % c, [P, PACK * n], BF16) for c, n in enumerate(CHUNKS)]
        hid_words = [sb("hid_words%d" % c, [P, n], U32) for c, n in enumerate(CHUNKS)]
        hid_scales = [sb("hid_scales%d" % c, [P, n], U8) for c, n in enumerate(CHUNKS)]
        res = [sb("res%d" % c, [P, PACK, n], F32) for c, n in enumerate(CHUNKS)]
        res_bf = [sb("res_bf%d" % c, [P, PACK * n], BF16) for c, n in enumerate(CHUNKS)]
        res_words = [sb("res_words%d" % c, [P, n], U32) for c, n in enumerate(CHUNKS)]
        res_scales = sb("res_scales", [P, U], U8)

        def entries(lst, c):
            return lst[:, starts[c] // 16 : (starts[c] + CHUNKS[c]) // 16]

        def fetch_z1(c, t):
            nc.scalar.activation(z_1[c][:, t, :], z[t][:].indirect(entries(el1_sb, c)), COPY)

        def fetch_z2(c, t):
            nc.scalar.activation(z_2[c][:, t, :], z[t][:].indirect(entries(el2_sb, c)), COPY)

        def make_rule(c, t):
            nc.vector.tensor_tensor(neg_rule[c][:, t, :], neg_y[t][:].indirect(entries(el2_sb, c)), z_1[c][:, t, :], ALU.mult)

        def take_larger(c, pair):
            ts = slice(2 * pair, 2 * pair + 2)
            nc.vector.scalar_tensor_tensor(larger[c][:, ts, :], neg_rule[c][:, ts, :], -1.0, z_2[c][:, ts, :], ALU.mult, ALU.max)

        def fetch_y1(c, t):
            nc.scalar.activation(neg_y_1[c][:, t, :], neg_y[t][:].indirect(entries(el1_sb, c)), COPY)

        def make_diff(c, pair):
            if 2 * c + pair < FUSED_STEPS:
                for t in (2 * pair, 2 * pair + 1):
                    nc.vector.tensor_tensor(diff[c][:, t, :], neg_y[t][:].indirect(entries(el1_sb, c)), larger[c][:, t, :], ALU.add)
            else:
                ts = slice(2 * pair, 2 * pair + 2)
                nc.vector.tensor_tensor(diff[c][:, ts, :], neg_y_1[c][:, ts, :], larger[c][:, ts, :], ALU.add)

        def scale_round(c):
            groups = CHUNKS[c] // RUN
            nc.vector.tensor_tensor(
                hid[c][:].rearrange("p (g i t) -> p g t i", i=RUN, t=PACK),
                diff[c][:].rearrange("p t (g i) -> p g t i", i=RUN),
                unit_sb[:].unsqueeze(1).unsqueeze(3).broadcast_to([P, groups, PACK, RUN]),
                ALU.mult,
            )

        def quantize_hid(c):
            nc.vector.quantize_mx(out=hid_words[c][:].bitcast(FP8X4), scales=hid_scales[c][:], in_=hid[c][:])

        out_rows = out_0.rearrange("(p t) r -> p t r", t=PACK)
        out_words = out_1[0].rearrange("p c r -> p (c r)").bitcast(I32)

        def properties(c, w3):
            for a in range(0, CHUNKS[c], UNIT):
                cols = slice(a, a + UNIT)
                bank = psum.tile([P, PACK, UNIT], F32, name="bank", tag="bank")
                for t in range(PACK):
                    words, scales = w3
                    nc.tensor.matmul_mx(
                        out=bank[:, t, :], lhsT=words[t, 0].bitcast(U8).bitcast(FP4X4), lhsT_scale=scales[t, 0],
                        rhs=hid_words[c][:, cols].bitcast(FP8X4), rhs_scale=hid_scales[c][:, cols],
                        start=True, stop=True,
                    )
                nc.scalar.copy(
                    res_bf[c][:, PACK * a : PACK * (a + UNIT)].rearrange("p (g i t) -> p g t i", i=RUN, t=PACK),
                    bank[:].rearrange("p t (g i) -> p g t i", i=RUN),
                )
                nc.scalar.copy(res[c][:, :, cols], bank[:])
            nc.sync.dma_start(out=out_rows[:, :, starts[c] : starts[c] + CHUNKS[c]], in_=res[c][:])

        def quantize_res(c, a):
            nc.vector.quantize_mx(
                out=res_words[c][:, a : a + UNIT].bitcast(FP8X4),
                scales=res_scales[:, starts[c] + a : starts[c] + a + UNIT],
                in_=res_bf[c][:, PACK * a : PACK * (a + UNIT)],
            )
            if a + UNIT == CHUNKS[c]:
                nc.sync.dma_start(out=out_words[:, starts[c] : starts[c] + CHUNKS[c]], in_=res_words[c][:].bitcast(I32))

        evac_z(0, False)
        evac_z(1, True)
        evac_y(0)
        evac_y(1)
        steps = [(c, pair) for c in range(len(CHUNKS)) for pair in range(2)]
        last = len(CHUNKS) - 1
        for j, (c, pair) in enumerate(steps):
            rows = (2 * pair, 2 * pair + 1)
            for t in rows:
                if j == 1:
                    evac_z(t, False)
                fetch_z1(c, t)
            for t in rows:
                fetch_z2(c, t)
            if j >= FUSED_STEPS:
                for t in rows:
                    fetch_y1(c, t)
            for t in rows:
                make_rule(c, t)
            if j == 0:
                evac_y(2)
                evac_y(3)
            if pair == 1 and c > 0:
                quantize_hid(c - 1)
                properties(c - 1, w3)
            if j > 0:
                make_diff(*steps[j - 1])
            take_larger(c, pair)
            if pair == 0 and c > 0:
                scale_round(c - 1)
            if j == 1:
                w3_dealt = sb("w3_dealt", [P, 3 * N], U8)
                w3 = (
                    deal(w3_dealt[:, : 2 * N].bitcast(U16), ww_raw[1][:].bitcast(U16), 1, 0, PACK),
                    deal(w3_dealt[:, 2 * N :], ws_raw[1][:], 1, 0, PACK),
                )
        quantize_res(0, 0)
        make_diff(last, 1)
        quantize_res(0, UNIT)
        scale_round(last)
        quantize_res(0, 2 * UNIT)
        quantize_hid(last)
        properties(last, w3)
        for c in range(1, len(CHUNKS)):
            for a in range(0, CHUNKS[c], UNIT):
                quantize_res(c, a)
        for q in range(QUADS):
            queue = nc.scalar if q % 2 else nc.sync
            queue.dma_start(
                out=out_2[0, 4 * q : 4 * q + 4, :].bitcast(I32), in_=res_scales[32 * q : 32 * q + 4, :].bitcast(I32)
            )
